import numpy as np
import ml_dtypes


def mxq(x, axis, fmt="e4m3"):
    dtype, down = {"e4m3": (ml_dtypes.float8_e4m3fn, 7), "e5m2": (ml_dtypes.float8_e5m2, 14)}[fmt]
    v = np.moveaxis(np.asarray(x, np.float32).astype(ml_dtypes.bfloat16).astype(np.float64), axis, -1)
    blocks = v.reshape(v.shape[:-1] + (-1, 32))
    amax = np.abs(blocks).max(-1, keepdims=True)
    byte = np.maximum(np.where(amax > 0, np.frexp(amax)[1] - 1 + 127, 0) - down, 1)
    scale = np.exp2(byte - 127.0)
    codes = (blocks / scale).astype(np.float32).astype(dtype).astype(np.float64)
    return np.moveaxis((codes * scale).reshape(v.shape), -1, axis)


WIDE = False


def mx_kscale(k):
    if not WIDE:
        return np.ones(k)
    levels = np.array([10, -10, 5, -5, 0])
    if k % 512:
        return np.exp2(np.random.permutation(np.resize(levels, k // 32))).repeat(32)
    a = np.empty((k // 512, 16))
    for p in range(k // 512):
        a[p, :8] = np.random.permutation(np.resize(levels, 8))
        for g in range(8):
            far = levels[np.abs(levels - a[p, g]) >= 10]
            a[p, g + 8] = far[np.random.randint(len(far))]
    return np.exp2(a.ravel()).repeat(32)


def f64(x):
    return np.asarray(x).astype(np.float64)


def striped(idx):
    return np.tile(np.asarray(idx).reshape(-1, 16).T, (8, 1)).astype(np.uint16)


def unstriped(offs):
    return offs[:16].T.reshape(-1).astype(np.int64)


E2M1 = np.array([0.0, 0.5, 1.0, 1.5, 2.0, 3.0, 4.0, 6.0, -0.0, -0.5, -1.0, -1.5, -2.0, -3.0, -4.0, -6.0])


def pack_weight(w, fmt):
    k, n = w.shape
    w = f64(np.asarray(w, np.float32).astype(ml_dtypes.bfloat16)).reshape(k // 32, 32, n)
    amax = np.abs(w).max(1)
    if fmt == "e4m3":
        byte = np.frexp(amax)[1] - 1 + 127 - 7
    else:
        mant, ex = np.frexp(amax / 6.0)
        byte = np.where(mant > 0.5, ex, ex - 1) + 127
    byte = np.clip(np.where(amax > 0, byte, 1), 1, 254)
    scaled = (w * np.exp2(127.0 - byte)[:, None, :]).reshape(k, n).astype(np.float32)
    by_word = np.ascontiguousarray(scaled.reshape(k // 512, 128, 4, n).transpose(0, 1, 3, 2))
    if fmt == "e4m3":
        words = by_word.astype(ml_dtypes.float8_e4m3fn).view(np.uint8)
    else:
        c = by_word.astype(ml_dtypes.float4_e2m1fn).view(np.uint8) & 0xF
        words = (c[..., 0::2] | (c[..., 1::2] << 4)).reshape(k // 512, 128, 2 * n)
    return np.ascontiguousarray(words), np.ascontiguousarray(byte.astype(np.uint8).reshape(k // 512, 16, n))


def unpack_weight(words, scales, fmt):
    g, _, n = scales.shape
    words = np.ascontiguousarray(words).reshape(g, 128, n, -1)
    if fmt == "e4m3":
        vals = words.view(ml_dtypes.float8_e4m3fn).astype(np.float64)
    else:
        nib = np.empty((g, 128, n, 4), np.uint8)
        nib[..., 0::2] = words & 0xF
        nib[..., 1::2] = words >> 4
        vals = E2M1[nib]
    vals = vals * np.repeat(np.exp2(scales.astype(np.float64) - 127.0), 8, axis=1)[..., None]
    return vals.transpose(0, 1, 3, 2).reshape(g * 512, n)


def sigmoid(v):
    return 1.0 / (1.0 + np.exp(-v))


def rot(x):
    y = x.reshape(-1, 2, x.shape[1])
    return np.stack([-y[:, 1], y[:, 0]], axis=1).reshape(x.shape)


K, R, F, T, J, U = 512, 512, 512, 2048, 256, 512


def setup_inputs():
    n = np.random.standard_normal
    idx = np.random.permutation(T)[:J]
    idx2 = np.random.randint(0, U, J)
    fk = mx_kscale(K)
    ff = mx_kscale(F)
    tabp = pack_weight(n((K, T)) / fk[:, None], "e2m1")
    dtabp = pack_weight(n((K, T)) / fk[:, None], "e2m1")
    return {
        "tab_words": tabp[0],
        "tab_scales": tabp[1],
        "w1": (n((K, R)) * 1 / np.sqrt(K) * fk[:, None]).astype(np.float32),
        "cosn": (np.repeat(np.round(np.cos(np.arange(R // 2)[:, None] * 0.11 + np.arange(U)[None] * 0.37) * 64) / 64, 2, axis=0)).astype(np.float32),
        "sinn": (np.repeat(np.round(np.sin(np.arange(R // 2)[:, None] * 0.11 + np.arange(U)[None] * 0.37) * 64) / 64, 2, axis=0)).astype(np.float32),
        "gain": (np.random.uniform(0.5, 1.5, (R, 1))).astype(np.float32),
        "wo": (n((F, R)) * 1 / np.sqrt(F) * ff[:, None]).astype(np.float32),
        "dy": (n((F, J)) / ff[:, None]).astype(np.float32),
        "dtab_words": dtabp[0],
        "dtab_scales": dtabp[1],
        "og": (np.random.uniform(0.7, 2.0, (R, 1))).astype(np.float32),
        "base": (0.3 * n((R, J))).astype(np.float32),
        "offs": striped(idx),
        "offs2": striped(idx2),
    }


def reference(tab_words, tab_scales, w1, cosn, sinn, gain, wo, dy, dtab_words, dtab_scales, og, base, offs, offs2):
    idx = unstriped(offs)
    idx2 = unstriped(offs2)
    tabu = unpack_weight(tab_words, tab_scales, "e2m1")
    dtabu = unpack_weight(dtab_words, dtab_scales, "e2m1")
    w1q = mxq(f64(w1), 0, "e4m3")
    tabidxg = tabu[:, idx]
    a = w1q.T @ tabidxg
    dtabidxg = dtabu[:, idx]
    ta = w1q.T @ dtabidxg
    o1 = rot(a)
    s = a * f64(cosn)[:, idx2] + o1 * f64(sinn)[:, idx2]
    s2 = s * f64(gain)
    woq = mxq(f64(wo), 0, "e4m3")
    dyq = mxq(f64(dy), 0, "e4m3")
    c0 = woq.T @ dyq
    xo1 = rot(ta)
    xs = ta * f64(cosn)[:, idx2] + xo1 * f64(sinn)[:, idx2]
    xs2 = xs * f64(gain)
    xds2 = (xs2 * sigmoid(s2) * (1.0 - sigmoid(s2)) * (1.0 + s2 * (1.0 - sigmoid(s2))) + (xs2 * (1.0 - sigmoid(s2)) + xs2 * sigmoid(s2) * (1.0 - sigmoid(s2)) * (-1.0) * s2) * sigmoid(s2)) * c0
    xds = xds2 * f64(gain)
    xdo1 = xds * f64(sinn)[:, idx2]
    xodo1 = rot(xdo1)
    xda = xds * f64(cosn)[:, idx2] - xodo1
    y = xda * f64(og) + f64(base)
    return y

@@ -1,0 +1,266 @@
+from contextlib import ExitStack
+
+import concourse.mybir as mybir
+from concourse.masks import make_identity
+
+F32 = mybir.dt.float32
+BF16 = mybir.dt.bfloat16
+I32 = mybir.dt.int32
+U32 = mybir.dt.uint32
+U16 = mybir.dt.uint16
+U8 = mybir.dt.uint8
+FP8X4 = mybir.dt.float8_e4m3fn_x4
+FP4X4 = mybir.dt.float4_e2m1fn_x4
+MULT = mybir.AluOpType.mult
+ADD = mybir.AluOpType.add
+SUB = mybir.AluOpType.subtract
+ACT = mybir.ActivationFunctionType
+
+P = 128
+K, R, T, J, U = 512, 512, 2048, 256, 512
+FLOPS = 3 * 2 * K * R * J
+POOL_M1 = (True, False)
+POOL_M4 = (True, False)
+POOL_R1 = (False, False)
+POOL_Y = (False, False)
+
+
+def tile_attend_hvturned_kernel(tc, tab_words, tab_scales, w1, cosn, sinn, gain, wo, dy, dtab_words, dtab_scales, og, base, offs, offs2, out):
+    nc = tc.nc
+    with ExitStack() as ctx:
+        keep = ctx.enter_context(tc.tile_pool(name="keep", bufs=1))
+        psum = ctx.enter_context(tc.psum_pool(name="psum", bufs=1))
+
+        def sb(name, shape, dtype=F32):
+            return keep.tile(shape, dtype, name=name, align_bytes=64)
+
+        offs_t = keep.tile([P, J // 16], U16, name="offs_t")
+        offs2_t = keep.tile([P, J // 16], U16, name="offs2_t")
+        words_win = [sb("words_win%d" % i, [P, T], U16) for i in range(2)]
+        scales_win = [sb("scales_win%d" % i, [P, T], U8) for i in range(2)]
+        cos_win = [sb("cos_win%d" % u, [P, U]) for u in range(2)]
+        sin_win = [sb("sin_win%d" % u, [P, U]) for u in range(2)]
+        w1_raw = [sb("w1_raw%d" % u, [P, 4, 256]) for u in range(2)]
+        wo_raw = [sb("wo_raw%d" % u, [P, 4, 256]) for u in range(2)]
+        dy_raw = sb("dy_raw", [P, 4, J])
+        base_t = [sb("base%d" % u, [P, 2, J]) for u in range(2)]
+        gain_t = sb("gain_t", [P, 2, 2])
+        og_t = sb("og_t", [P, 2, 2])
+        ident = sb("ident", [P, P])
+
+        for i in range(2):
+            nc.vector.memset(scales_win[i][:].bitcast(I32), 0)
+
+        def load_scales(i, src):
+            for r in range(4):
+                nc.sync.dma_start(out=scales_win[i][r:P:32, :].bitcast(I32), in_=src[0, r:16:4, :].bitcast(I32))
+
+        def load_half(dst, src, u):
+            nc.sync.dma_start(out=dst[:], in_=src[:, 256 * u : 256 * (u + 1)].rearrange("(p j) c -> p j c", j=4))
+
+        def load_angles(dst, src, u):
+            nc.sync.dma_start(out=dst[:], in_=src[256 * u : 256 * (u + 1), :].rearrange("(p e) c -> p e c", e=2)[:, 0, :])
+
+        nc.sync.dma_start(offs_t[:], offs)
+        load_half(w1_raw[0], w1, 0)
+        load_scales(0, tab_scales)
+        nc.sync.dma_start(out=words_win[0][:].bitcast(I32), in_=tab_words[0].bitcast(I32))
+        nc.sync.dma_start(offs2_t[:], offs2)
+        load_scales(1, dtab_scales)
+        nc.gpsimd.dma_start(out=gain_t[:], in_=gain.rearrange("(u p e) o -> p u (e o)", u=2, e=2))
+        nc.gpsimd.dma_start(out=og_t[:], in_=og.rearrange("(u p e) o -> p u (e o)", u=2, e=2))
+        load_angles(cos_win[0], cosn, 0)
+        load_angles(sin_win[0], sinn, 0)
+        nc.sync.dma_start(out=words_win[1][:].bitcast(I32), in_=dtab_words[0].bitcast(I32))
+        load_half(w1_raw[1], w1, 1)
+        load_angles(cos_win[1], cosn, 1)
+        load_angles(sin_win[1], sinn, 1)
+        nc.sync.dma_start(out=dy_raw[:], in_=dy.rearrange("(p j) c -> p j c", j=4))
+        load_half(wo_raw[0], wo, 0)
+        load_half(wo_raw[1], wo, 1)
+        for u in range(2):
+            nc.sync.dma_start(out=base_t[u][:], in_=base[256 * u : 256 * (u + 1), :].rearrange("(p e) c -> p e c", e=2))
+
+        make_identity(nc, ident[:])
+        warm = sb("warm", [P, 1])
+        warm_in = sb("warm_in", [P, 1])
+        nc.vector.memset(warm_in[:], 0.0)
+        nc.scalar.activation(warm[:], warm_in[:], ACT.Tanh)
+
+        fac = [sb("fac%d" % i, [P, 4]) for i in range(2)]
+        nfac = [sb("nfac%d" % i, [P, 4]) for i in range(2)]
+        g4 = gain_t[:].rearrange("p u e -> p (u e)")
+        nc.gpsimd.tensor_scalar(fac[0][:], g4, 0.5, 0.0, MULT, ADD)
+        nc.gpsimd.tensor_scalar(nfac[0][:], g4, -0.5, 0.0, MULT, ADD)
+        nc.gpsimd.tensor_tensor(fac[1][:], fac[0][:], g4, MULT)
+        nc.gpsimd.tensor_tensor(nfac[1][:], nfac[0][:], g4, MULT)
+
+        def cast_dealt(name, raw):
+            grouped = sb(name + "_bf", [P, 1024], BF16)
+            nc.scalar.copy(
+                grouped[:].rearrange("p (e m i j) -> p m j i e", e=2, i=2, j=4),
+                raw[:].rearrange("p j (m i e) -> p m j i e", i=2, e=2),
+            )
+            return grouped
+
+        def cast_plain(name, raw):
+            grouped = sb(name + "_bf", [P, 1024], BF16)
+            nc.scalar.copy(
+                grouped[:].rearrange("p (c i j) -> p c j i", i=4, j=4),
+                raw[:].rearrange("p j (c i) -> p c j i", i=4),
+            )
+            return grouped
+
+        def quantize(name, grouped):
+            codes = sb(name + "_codes", [P, 256], U32)
+            scales = sb(name + "_scales", [P, 256], U8)
+            nc.vector.quantize_mx(out=codes[:].bitcast(FP8X4), scales=scales[:], in_=grouped[:])
+            return codes, scales
+
+        def gather(name, win, lst, dtype):
+            got = sb(name, [P, J], dtype)
+            nc.vector.tensor_copy(got[:], win[:].indirect(lst[:]))
+            return got
+
+        def first_layer(wq, words, scales):
+            bank = psum.tile([P, 2, J], F32, name="mm", tag="mm", bufs=2)
+            for e in range(2):
+                cols = slice(P * e, P * (e + 1))
+                nc.tensor.matmul_mx(out=bank[:, e, :], lhsT=wq[0][:, cols].bitcast(FP8X4), lhsT_scale=wq[1][:, cols],
+                                    rhs=words[:].bitcast(FP4X4), rhs_scale=scales[:], start=True, stop=True)
+            return bank
+
+        def turned_sum(dst, a, b):
+            nc.tensor.matmul(dst, lhsT=a, rhs=ident[:], is_transpose=True, start=True, stop=False)
+            nc.tensor.matmul(dst, lhsT=b, rhs=ident[:], is_transpose=True, start=False, stop=True)
+
+        def forward(name, i, u, bank, c, s):
+            dst = psum.tile([P, 2, 2, P], F32, name="rot%d" % i, tag="rot%d" % i, bufs=1 + i)
+            for e in range(2):
+                col = slice(2 * u + e, 2 * u + e + 1)
+                pc = sb("%s_c%d" % (name, e), [P, J])
+                ps = sb("%s_s%d" % (name, e), [P, J])
+                nc.vector.scalar_tensor_tensor(pc[:], bank[:, e, :], fac[i][:, col], c[:], MULT, MULT)
+                nc.vector.scalar_tensor_tensor(ps[:], bank[:, 1 - e, :], (nfac if e == 0 else fac)[i][:, col], s[:], MULT, MULT)
+                for jb in range(2):
+                    js = slice(P * jb, P * (jb + 1))
+                    turned_sum(dst[:, jb, e, :], pc[:, js], ps[:, js])
+            return dst
+
+        def turn_angles(c, s):
+            dst = psum.tile([P, 2, 2, P], F32, name="cs", tag="cs", bufs=2)
+            for k, src in enumerate((c, s)):
+                for jb in range(2):
+                    nc.tensor.transpose(dst[:, k, jb, :], src[:, P * jb : P * (jb + 1)], ident[:])
+            return dst
+
+        def flat(t):
+            return t[:].rearrange("p a b c -> p (a b c)")
+
+        def curve(u, h):
+            t = sb("t%d" % u, [P, 512])
+            q = sb("q%d" % u, [P, 512])
+            ht = sb("ht%d" % u, [P, 512])
+            nc.scalar.activation(t[:], flat(h), ACT.Tanh)
+            if POOL_M1[u]:
+                hs = sb("hs%d" % u, [P, 512])
+                nc.scalar.copy(hs[:], flat(h))
+                nc.gpsimd.tensor_tensor(ht[:], hs[:], t[:], MULT)
+            else:
+                nc.vector.tensor_tensor(ht[:], flat(h), t[:], MULT)
+            nc.scalar.activation(q[:], t[:], ACT.Square)
+            return q, ht
+
+        def last_layer(dyq, woq):
+            bank = psum.tile([P, 2, 256], F32, name="c0", tag="c0", bufs=1)
+            for jb in range(2):
+                cols = slice(P * jb, P * (jb + 1))
+                nc.tensor.matmul_mx(out=bank[:, jb, :], lhsT=dyq[0][:, cols].bitcast(FP8X4), lhsT_scale=dyq[1][:, cols],
+                                    rhs=woq[0][:].bitcast(FP8X4), rhs_scale=woq[1][:], start=True, stop=True)
+            return bank
+
+        def m3(u, ht, xs):
+            w2 = sb("w2_%d" % u, [P, 512])
+            nc.vector.scalar_tensor_tensor(w2[:], ht[:], 1.0, flat(xs), SUB, MULT)
+            return w2
+
+        def m2(u, q, c0):
+            wa = sb("wa_%d" % u, [P, 512])
+            nc.vector.scalar_tensor_tensor(wa[:], q[:], 1.0, c0[:].rearrange("p a b -> p (a b)"), SUB, MULT)
+            return wa
+
+        def m4(u, wa, w2):
+            x = sb("x%d" % u, [P, 2, 2, P])
+            (nc.gpsimd if POOL_M4[u] else nc.vector).tensor_tensor(flat(x), wa[:], w2[:], MULT)
+            return x
+
+        def back(u, x, cs):
+            rc = sb("rc%d" % u, [P, 2, 2, P])
+            rs = [sb("rs%d_%d" % (u, e), [P, 2, P]) for e in range(2)]
+            nc.vector.tensor_tensor(rs[0][:], x[:, :, 1, :], cs[:, 1, :, :], MULT)
+            nc.vector.scalar_tensor_tensor(rs[1][:], x[:, :, 0, :], -1.0, cs[:, 1, :, :], MULT, MULT)
+            if POOL_R1[u]:
+                ct = sb("ct%d" % u, [P, 2, P])
+                nc.scalar.copy(ct[:], cs[:, 0, :, :])
+                nc.gpsimd.tensor_tensor(rc[:], x[:], ct[:].unsqueeze(2).to_broadcast([P, 2, 2, P]), MULT)
+            else:
+                nc.vector.tensor_tensor(rc[:], x[:], cs[:, 0, :, :].unsqueeze(2).to_broadcast([P, 2, 2, P]), MULT)
+            y = psum.tile([P, 2, J], F32, name="mm", tag="mm", bufs=2)
+            for e in range(2):
+                for jb in range(2):
+                    turned_sum(y[:, e, P * jb : P * (jb + 1)], rs[e][:, jb, :], rc[:, jb, e, :])
+            return y
+
+        def finish(u, y):
+            res = sb("res%d" % u, [P, 2, J])
+            for e in range(2):
+                if POOL_Y[u]:
+                    tmp = sb("ytmp%d_%d" % (u, e), [P, J])
+                    nc.scalar.activation(tmp[:], y[:, e, :], ACT.Copy, scale=og_t[:, u, e : e + 1])
+                    nc.gpsimd.tensor_tensor(res[:, e, :], tmp[:], base_t[u][:, e, :], ADD)
+                else:
+                    nc.vector.scalar_tensor_tensor(res[:, e, :], y[:, e, :], og_t[:, u, e : e + 1], base_t[u][:, e, :], MULT, ADD)
+            nc.sync.dma_start(out=out[256 * u : 256 * (u + 1), :].rearrange("(p e) c -> p e c", e=2), in_=res[:])
+
+        w1b0 = cast_dealt("w1_0", w1_raw[0])
+        sc0 = gather("sc0", scales_win[0], offs_t, U8)
+        w1q0 = quantize("w1_0", w1b0)
+        wd0 = gather("wd0", words_win[0], offs_t, U16)
+        a0 = first_layer(w1q0, wd0, sc0)
+        c_0 = gather("c_0", cos_win[0], offs2_t, F32)
+        s_0 = gather("s_0", sin_win[0], offs2_t, F32)
+        sc1 = gather("sc1", scales_win[1], offs_t, U8)
+        wd1 = gather("wd1", words_win[1], offs_t, U16)
+        t0 = first_layer(w1q0, wd1, sc1)
+        h0 = forward("fa0", 0, 0, a0, c_0, s_0)
+        w1b1 = cast_dealt("w1_1", w1_raw[1])
+        w1q1 = quantize("w1_1", w1b1)
+        x0 = forward("ft0", 1, 0, t0, c_0, s_0)
+        q0, ht0 = curve(0, h0)
+        a1 = first_layer(w1q1, wd0, sc0)
+        c_1 = gather("c_1", cos_win[1], offs2_t, F32)
+        s_1 = gather("s_1", sin_win[1], offs2_t, F32)
+        t1 = first_layer(w1q1, wd1, sc1)
+        cs0 = turn_angles(c_0, s_0)
+        dyb = cast_plain("dy", dy_raw)
+        wob0 = cast_dealt("wo_0", wo_raw[0])
+        h1 = forward("fa1", 0, 1, a1, c_1, s_1)
+        w20 = m3(0, ht0, x0)
+        dyq = quantize("dy", dyb)
+        woq0 = quantize("wo_0", wob0)
+        c00 = last_layer(dyq, woq0)
+        x1 = forward("ft1", 1, 1, t1, c_1, s_1)
+        q1, ht1 = curve(1, h1)
+        wob1 = cast_dealt("wo_1", wo_raw[1])
+        wa0 = m2(0, q0, c00)
+        xx0 = m4(0, wa0, w20)
+        cs1 = turn_angles(c_1, s_1)
+        woq1 = quantize("wo_1", wob1)
+        c01 = last_layer(dyq, woq1)
+        w21 = m3(1, ht1, x1)
+        wa1 = m2(1, q1, c01)
+        y0 = back(0, xx0, cs0)
+        xx1 = m4(1, wa1, w21)
+        y1 = back(1, xx1, cs1)
+        finish(0, y0)
+        finish(1, y1)

@@ -17,22 +17,34 @@ SUB = mybir.AluOpType.subtract
 ACT = mybir.ActivationFunctionType
 
 P = 128
+PACK = 4
 K, R, T, J, U = 512, 512, 2048, 256, 512
+HALF = R // 2
+SCALE_ROWS = K // 32
+BANK = 512
+
 FLOPS = 3 * 2 * K * R * J
-POOL_M1 = (True, False)
-POOL_M4 = (True, False)
-POOL_R1 = (False, False)
-POOL_Y = (False, False)
 
 
-def tile_attend_hvturned_kernel(tc, tab_words, tab_scales, w1, cosn, sinn, gain, wo, dy, dtab_words, dtab_scales, og, base, offs, offs2, out):
+def tile_attend_hvturned_kernel(
+    tc, tab_words, tab_scales, w1, cosn, sinn, gain, wo, dy, dtab_words, dtab_scales, og, base, offs, offs2, out
+):
     nc = tc.nc
     with ExitStack() as ctx:
         keep = ctx.enter_context(tc.tile_pool(name="keep", bufs=1))
         psum = ctx.enter_context(tc.psum_pool(name="psum", bufs=1))
 
-        def sb(name, shape, dtype=F32):
-            return keep.tile(shape, dtype, name=name, align_bytes=64)
+        def sb(name, shape, dtype=F32, reuse=None):
+            return keep.tile(shape, dtype, name=name, tag=reuse or name, align_bytes=64)
+
+        def bank(letter, shape):
+            return psum.tile(shape, F32, name="bank" + letter, tag="bank" + letter)
+
+        def flat(tile):
+            return tile[:].rearrange("p a b c -> p (a b c)")
+
+        def half_rows(src, u):
+            return src[HALF * u : HALF * (u + 1), :].rearrange("(p e) c -> p e c", e=2)
 
         offs_t = keep.tile([P, J // 16], U16, name="offs_t")
         offs2_t = keep.tile([P, J // 16], U16, name="offs2_t")
@@ -40,227 +52,238 @@ def tile_attend_hvturned_kernel(tc, tab_words, tab_scales, w1, cosn, sinn, gain,
         scales_win = [sb("scales_win%d" % i, [P, T], U8) for i in range(2)]
         cos_win = [sb("cos_win%d" % u, [P, U]) for u in range(2)]
         sin_win = [sb("sin_win%d" % u, [P, U]) for u in range(2)]
-        w1_raw = [sb("w1_raw%d" % u, [P, 4, 256]) for u in range(2)]
-        wo_raw = [sb("wo_raw%d" % u, [P, 4, 256]) for u in range(2)]
-        dy_raw = sb("dy_raw", [P, 4, J])
+        w1_raw = [sb("w1_raw%d" % u, [P, PACK, HALF]) for u in range(2)]
+        wo_raw = [sb("wo_raw%d" % u, [P, PACK, HALF]) for u in range(2)]
+        dy_raw = sb("dy_raw", [P, PACK, J])
         base_t = [sb("base%d" % u, [P, 2, J]) for u in range(2)]
         gain_t = sb("gain_t", [P, 2, 2])
         og_t = sb("og_t", [P, 2, 2])
         ident = sb("ident", [P, P])
 
-        for i in range(2):
-            nc.vector.memset(scales_win[i][:].bitcast(I32), 0)
+        nc.gpsimd.memset(scales_win[0][:].bitcast(I32), 0)
+        nc.vector.memset(scales_win[1][:].bitcast(I32), 0)
+
+        def load_words(i, src):
+            nc.sync.dma_start(out=words_win[i][:].bitcast(I32), in_=src[0].bitcast(I32))
 
         def load_scales(i, src):
             for r in range(4):
-                nc.sync.dma_start(out=scales_win[i][r:P:32, :].bitcast(I32), in_=src[0, r:16:4, :].bitcast(I32))
+                nc.sync.dma_start(out=scales_win[i][r:P:32, :].bitcast(I32), in_=src[0, r:SCALE_ROWS:4, :].bitcast(I32))
 
-        def load_half(dst, src, u):
-            nc.sync.dma_start(out=dst[:], in_=src[:, 256 * u : 256 * (u + 1)].rearrange("(p j) c -> p j c", j=4))
+        def load_operand(dst, src):
+            nc.sync.dma_start(out=dst[:], in_=src.rearrange("(p j) c -> p j c", j=PACK))
+
+        def load_weights(dst, src, u):
+            load_operand(dst[u], src[:, HALF * u : HALF * (u + 1)])
 
         def load_angles(dst, src, u):
-            nc.sync.dma_start(out=dst[:], in_=src[256 * u : 256 * (u + 1), :].rearrange("(p e) c -> p e c", e=2)[:, 0, :])
+            nc.sync.dma_start(out=dst[u][:], in_=half_rows(src, u)[:, 0, :])
+
+        def load_per_feature(dst, src):
+            nc.sync.dma_start(out=dst[:], in_=src.rearrange("(u p e) o -> p u (e o)", u=2, e=2))
 
         nc.sync.dma_start(offs_t[:], offs)
-        load_half(w1_raw[0], w1, 0)
-        load_scales(0, tab_scales)
-        nc.sync.dma_start(out=words_win[0][:].bitcast(I32), in_=tab_words[0].bitcast(I32))
         nc.sync.dma_start(offs2_t[:], offs2)
-        load_scales(1, dtab_scales)
-        nc.gpsimd.dma_start(out=gain_t[:], in_=gain.rearrange("(u p e) o -> p u (e o)", u=2, e=2))
-        nc.gpsimd.dma_start(out=og_t[:], in_=og.rearrange("(u p e) o -> p u (e o)", u=2, e=2))
-        load_angles(cos_win[0], cosn, 0)
-        load_angles(sin_win[0], sinn, 0)
-        nc.sync.dma_start(out=words_win[1][:].bitcast(I32), in_=dtab_words[0].bitcast(I32))
-        load_half(w1_raw[1], w1, 1)
-        load_angles(cos_win[1], cosn, 1)
-        load_angles(sin_win[1], sinn, 1)
-        nc.sync.dma_start(out=dy_raw[:], in_=dy.rearrange("(p j) c -> p j c", j=4))
-        load_half(wo_raw[0], wo, 0)
-        load_half(wo_raw[1], wo, 1)
-        for u in range(2):
-            nc.sync.dma_start(out=base_t[u][:], in_=base[256 * u : 256 * (u + 1), :].rearrange("(p e) c -> p e c", e=2))
-
+        load_scales(0, tab_scales)
         make_identity(nc, ident[:])
-        warm = sb("warm", [P, 1])
-        warm_in = sb("warm_in", [P, 1])
-        nc.vector.memset(warm_in[:], 0.0)
-        nc.scalar.activation(warm[:], warm_in[:], ACT.Tanh)
+        load_weights(w1_raw, w1, 0)
+        load_words(0, tab_words)
+        load_scales(1, dtab_scales)
+        load_per_feature(gain_t, gain)
+        load_words(1, dtab_words)
+        load_angles(cos_win, cosn, 0)
+        load_angles(sin_win, sinn, 0)
+        load_weights(w1_raw, w1, 1)
+        load_operand(dy_raw, dy)
+        load_weights(wo_raw, wo, 0)
+        load_angles(cos_win, cosn, 1)
+        load_angles(sin_win, sinn, 1)
+        load_weights(wo_raw, wo, 1)
+        load_per_feature(og_t, og)
+        for u in range(2):
+            nc.sync.dma_start(out=base_t[u][:], in_=half_rows(base, u))
 
-        fac = [sb("fac%d" % i, [P, 4]) for i in range(2)]
-        nfac = [sb("nfac%d" % i, [P, 4]) for i in range(2)]
-        g4 = gain_t[:].rearrange("p u e -> p (u e)")
-        nc.gpsimd.tensor_scalar(fac[0][:], g4, 0.5, 0.0, MULT, ADD)
-        nc.gpsimd.tensor_scalar(nfac[0][:], g4, -0.5, 0.0, MULT, ADD)
-        nc.gpsimd.tensor_tensor(fac[1][:], fac[0][:], g4, MULT)
-        nc.gpsimd.tensor_tensor(nfac[1][:], nfac[0][:], g4, MULT)
+        def gain_factors():
+            lin, neg_lin, sq, neg_sq = [sb(name, [P, 2, 2]) for name in ("lin", "neg_lin", "sq", "neg_sq")]
+            nc.scalar.activation(lin[:], gain_t[:], ACT.Copy, scale=0.5)
+            nc.scalar.activation(neg_lin[:], gain_t[:], ACT.Copy, scale=-0.5)
+            nc.scalar.activation(sq[:], gain_t[:], ACT.Square, scale=0.5**0.5)
+            nc.scalar.activation(neg_sq[:], sq[:], ACT.Copy, scale=-1.0)
+            return (lin, neg_lin), (sq, neg_sq)
 
-        def cast_dealt(name, raw):
-            grouped = sb(name + "_bf", [P, 1024], BF16)
+        def cast_weights(name, raw):
+            grouped = sb(name + "_bf", [P, PACK * HALF], BF16)
             nc.scalar.copy(
-                grouped[:].rearrange("p (e m i j) -> p m j i e", e=2, i=2, j=4),
+                grouped[:].rearrange("p (e m i j) -> p m j i e", e=2, i=2, j=PACK),
                 raw[:].rearrange("p j (m i e) -> p m j i e", i=2, e=2),
             )
             return grouped
 
-        def cast_plain(name, raw):
-            grouped = sb(name + "_bf", [P, 1024], BF16)
+        def cast_dy():
+            grouped = sb("dy_bf", [P, PACK * J], BF16)
             nc.scalar.copy(
-                grouped[:].rearrange("p (c i j) -> p c j i", i=4, j=4),
-                raw[:].rearrange("p j (c i) -> p c j i", i=4),
+                grouped[:].rearrange("p (c i j) -> p c j i", i=4, j=PACK),
+                dy_raw[:].rearrange("p j (c i) -> p c j i", i=4),
             )
             return grouped
 
-        def quantize(name, grouped):
-            codes = sb(name + "_codes", [P, 256], U32)
-            scales = sb(name + "_scales", [P, 256], U8)
+        def quantize(name, grouped, reuse=None):
+            width = grouped.shape[1] // PACK
+            codes = sb(name + "_codes", [P, width], U32, reuse)
+            scales = sb(name + "_scales", [P, width], U8)
             nc.vector.quantize_mx(out=codes[:].bitcast(FP8X4), scales=scales[:], in_=grouped[:])
             return codes, scales
 
-        def gather(name, win, lst, dtype):
+        def gather(name, window, offsets, dtype):
             got = sb(name, [P, J], dtype)
-            nc.vector.tensor_copy(got[:], win[:].indirect(lst[:]))
+            nc.vector.tensor_copy(got[:], window[:].indirect(offsets[:]))
             return got
 
-        def first_layer(wq, words, scales):
-            bank = psum.tile([P, 2, J], F32, name="mm", tag="mm", bufs=2)
-            for e in range(2):
-                cols = slice(P * e, P * (e + 1))
-                nc.tensor.matmul_mx(out=bank[:, e, :], lhsT=wq[0][:, cols].bitcast(FP8X4), lhsT_scale=wq[1][:, cols],
-                                    rhs=words[:].bitcast(FP4X4), rhs_scale=scales[:], start=True, stop=True)
-            return bank
+        def product(letter, stationary, moving, moving_dtype):
+            acc = bank(letter, [P, 2, BANK // 2])
+            for b in range(2):
+                cols = slice(P * b, P * (b + 1))
+                nc.tensor.matmul_mx(
+                    out=acc[:, b, :],
+                    lhsT=stationary[0][:, cols].bitcast(FP8X4),
+                    lhsT_scale=stationary[1][:, cols],
+                    rhs=moving[0][:].bitcast(moving_dtype),
+                    rhs_scale=moving[1][:],
+                    start=True,
+                    stop=True,
+                )
+            return acc
 
-        def turned_sum(dst, a, b):
-            nc.tensor.matmul(dst, lhsT=a, rhs=ident[:], is_transpose=True, start=True, stop=False)
-            nc.tensor.matmul(dst, lhsT=b, rhs=ident[:], is_transpose=True, start=False, stop=True)
+        def transpose_term(dsts, srcs, opens=False, closes=False):
+            last = len(dsts) - 1
+            for n, (dst, src) in enumerate(zip(dsts, srcs)):
+                nc.tensor.matmul(
+                    dst, lhsT=src, rhs=ident[:], is_transpose=True, start=opens and n == 0, stop=closes and n == last
+                )
 
-        def forward(name, i, u, bank, c, s):
-            dst = psum.tile([P, 2, 2, P], F32, name="rot%d" % i, tag="rot%d" % i, bufs=1 + i)
+        def slot_blocks(ap):
+            return [ap[:, P * jb : P * (jb + 1)] for jb in range(2)]
+
+        def turn_forward(name, letter, u, acc, factors, cos, sin, reuse=None):
+            plus, minus = factors
+            dst = bank(letter, [P, 2, 2, P])
+            prod = sb(name, [P, 2, 2, J], reuse=reuse)
+            regions = [[dst[:, jb, e, :] for jb in range(2)] for e in range(2)]
             for e in range(2):
-                col = slice(2 * u + e, 2 * u + e + 1)
-                pc = sb("%s_c%d" % (name, e), [P, J])
-                ps = sb("%s_s%d" % (name, e), [P, J])
-                nc.vector.scalar_tensor_tensor(pc[:], bank[:, e, :], fac[i][:, col], c[:], MULT, MULT)
-                nc.vector.scalar_tensor_tensor(ps[:], bank[:, 1 - e, :], (nfac if e == 0 else fac)[i][:, col], s[:], MULT, MULT)
-                for jb in range(2):
-                    js = slice(P * jb, P * (jb + 1))
-                    turned_sum(dst[:, jb, e, :], pc[:, js], ps[:, js])
+                nc.vector.scalar_tensor_tensor(prod[:, e, 0, :], acc[:, e, :], plus[:, u, e : e + 1], cos[:], MULT, MULT)
+                transpose_term(regions[e], slot_blocks(prod[:, e, 0, :]), opens=e == 0)
+            for e, sin_factor in enumerate((minus, plus)):
+                nc.vector.scalar_tensor_tensor(
+                    prod[:, e, 1, :], acc[:, 1 - e, :], sin_factor[:, u, e : e + 1], sin[:], MULT, MULT
+                )
+                transpose_term(regions[e], slot_blocks(prod[:, e, 1, :]), closes=e == 1)
             return dst
 
-        def turn_angles(c, s):
-            dst = psum.tile([P, 2, 2, P], F32, name="cs", tag="cs", bufs=2)
-            for k, src in enumerate((c, s)):
-                for jb in range(2):
-                    nc.tensor.transpose(dst[:, k, jb, :], src[:, P * jb : P * (jb + 1)], ident[:])
+        def angles_to_slot_layout(cos, sin):
+            dst = bank("G", [P, 2, 2, P])
+            for k, src in enumerate((cos, sin)):
+                for jb, block in enumerate(slot_blocks(src)):
+                    nc.tensor.transpose(dst[:, k, jb, :], block, ident[:])
             return dst
 
-        def flat(t):
-            return t[:].rearrange("p a b c -> p (a b c)")
+        def minus_one_times(name, tile, acc):
+            dst = sb(name, [P, BANK])
+            nc.vector.scalar_tensor_tensor(dst[:], tile[:], 1.0, acc, SUB, MULT)
+            return dst
 
-        def curve(u, h):
-            t = sb("t%d" % u, [P, 512])
-            q = sb("q%d" % u, [P, 512])
-            ht = sb("ht%d" % u, [P, 512])
-            nc.scalar.activation(t[:], flat(h), ACT.Tanh)
-            if POOL_M1[u]:
-                hs = sb("hs%d" % u, [P, 512])
-                nc.scalar.copy(hs[:], flat(h))
-                nc.gpsimd.tensor_tensor(ht[:], hs[:], t[:], MULT)
-            else:
-                nc.vector.tensor_tensor(ht[:], flat(h), t[:], MULT)
-            nc.scalar.activation(q[:], t[:], ACT.Square)
-            return q, ht
+        def add_base(res, u, e, xda):
+            nc.vector.scalar_tensor_tensor(res[:, e, :], xda[:, e, :], og_t[:, u, e : e + 1], base_t[u][:, e, :], MULT, ADD)
 
-        def last_layer(dyq, woq):
-            bank = psum.tile([P, 2, 256], F32, name="c0", tag="c0", bufs=1)
-            for jb in range(2):
-                cols = slice(P * jb, P * (jb + 1))
-                nc.tensor.matmul_mx(out=bank[:, jb, :], lhsT=dyq[0][:, cols].bitcast(FP8X4), lhsT_scale=dyq[1][:, cols],
-                                    rhs=woq[0][:].bitcast(FP8X4), rhs_scale=woq[1][:], start=True, stop=True)
-            return bank
+        tab_sc = gather("tab_sc", scales_win[0], offs_t, U8)
+        w1_bf0 = cast_weights("w1_0", w1_raw[0])
+        h_factors, xs_factors = gain_factors()
+        tab = (gather("tab_wd", words_win[0], offs_t, U16), tab_sc)
+        w1q0 = quantize("w1_0", w1_bf0)
+        a0 = product("A", w1q0, tab, FP4X4)
+        dtab_sc = gather("dtab_sc", scales_win[1], offs_t, U8)
+        dtab = (gather("dtab_wd", words_win[1], offs_t, U16), dtab_sc)
+        ta0 = product("B", w1q0, dtab, FP4X4)
+        cos0 = gather("cos0", cos_win[0], offs2_t, F32)
+        sin0 = gather("sin0", sin_win[0], offs2_t, F32)
+        h0 = turn_forward("h_prod0", "C", 0, a0, h_factors, cos0, sin0)
+        w1_bf1 = cast_weights("w1_1", w1_raw[1])
+        xs0 = turn_forward("xs_prod0", "D", 0, ta0, xs_factors, cos0, sin0)
 
-        def m3(u, ht, xs):
-            w2 = sb("w2_%d" % u, [P, 512])
-            nc.vector.scalar_tensor_tensor(w2[:], ht[:], 1.0, flat(xs), SUB, MULT)
-            return w2
+        w1q1 = quantize("w1_1", w1_bf1)
+        a1 = product("A", w1q1, tab, FP4X4)
+        ta1 = product("B", w1q1, dtab, FP4X4)
+        angles0 = angles_to_slot_layout(cos0, sin0)
+        dy_bf = cast_dy()
+        wo_bf0 = cast_weights("wo_0", wo_raw[0])
 
-        def m2(u, q, c0):
-            wa = sb("wa_%d" % u, [P, 512])
-            nc.vector.scalar_tensor_tensor(wa[:], q[:], 1.0, c0[:].rearrange("p a b -> p (a b)"), SUB, MULT)
-            return wa
+        t_and_h0 = sb("t_and_h0", [P, 2, BANK], reuse="wo_raw0")
+        tt0 = sb("tt0", [P, BANK])
+        ht0 = sb("ht0", [P, BANK])
+        nc.scalar.activation(t_and_h0[:, 0, :], flat(h0), ACT.Tanh)
+        nc.scalar.copy(t_and_h0[:, 1, :], flat(h0))
+        nc.gpsimd.tensor_tensor(ht0[:], t_and_h0[:, 1, :], t_and_h0[:, 0, :], MULT)
+        nc.scalar.activation(tt0[:], t_and_h0[:, 0, :], ACT.Square)
 
-        def m4(u, wa, w2):
-            x = sb("x%d" % u, [P, 2, 2, P])
-            (nc.gpsimd if POOL_M4[u] else nc.vector).tensor_tensor(flat(x), wa[:], w2[:], MULT)
-            return x
+        dyq = quantize("dy", dy_bf)
+        cos1 = gather("cos1", cos_win[1], offs2_t, F32)
+        woq0 = quantize("wo_0", wo_bf0, reuse="cos_win1")
+        c0_0 = product("F", dyq, woq0, FP8X4)
+        sin1 = gather("sin1", sin_win[1], offs2_t, F32)
+        h1 = turn_forward("h_prod1", "C", 1, a1, h_factors, cos1, sin1, reuse="wo_0_bf")
+        wo_bf1 = cast_weights("wo_1", wo_raw[1])
 
-        def back(u, x, cs):
-            rc = sb("rc%d" % u, [P, 2, 2, P])
-            rs = [sb("rs%d_%d" % (u, e), [P, 2, P]) for e in range(2)]
-            nc.vector.tensor_tensor(rs[0][:], x[:, :, 1, :], cs[:, 1, :, :], MULT)
-            nc.vector.scalar_tensor_tensor(rs[1][:], x[:, :, 0, :], -1.0, cs[:, 1, :, :], MULT, MULT)
-            if POOL_R1[u]:
-                ct = sb("ct%d" % u, [P, 2, P])
-                nc.scalar.copy(ct[:], cs[:, 0, :, :])
-                nc.gpsimd.tensor_tensor(rc[:], x[:], ct[:].unsqueeze(2).to_broadcast([P, 2, 2, P]), MULT)
-            else:
-                nc.vector.tensor_tensor(rc[:], x[:], cs[:, 0, :, :].unsqueeze(2).to_broadcast([P, 2, 2, P]), MULT)
-            y = psum.tile([P, 2, J], F32, name="mm", tag="mm", bufs=2)
-            for e in range(2):
-                for jb in range(2):
-                    turned_sum(y[:, e, P * jb : P * (jb + 1)], rs[e][:, jb, :], rc[:, jb, e, :])
-            return y
+        cos_slot0 = sb("cos_slot0", [P, 2, P], reuse="wo_raw0")
+        sin_slot0 = sb("sin_slot0", [P, 2, 2, P], reuse="wo_raw1")
+        nc.scalar.copy(cos_slot0[:], angles0[:, 0, :, :])
+        nc.scalar.activation(sin_slot0[:, :, 0, :], angles0[:, 1, :, :], ACT.Copy, scale=-1.0)
+        nc.scalar.copy(sin_slot0[:, :, 1, :], angles0[:, 1, :, :])
 
-        def finish(u, y):
-            res = sb("res%d" % u, [P, 2, J])
-            for e in range(2):
-                if POOL_Y[u]:
-                    tmp = sb("ytmp%d_%d" % (u, e), [P, J])
-                    nc.scalar.activation(tmp[:], y[:, e, :], ACT.Copy, scale=og_t[:, u, e : e + 1])
-                    nc.gpsimd.tensor_tensor(res[:, e, :], tmp[:], base_t[u][:, e, :], ADD)
-                else:
-                    nc.vector.scalar_tensor_tensor(res[:, e, :], y[:, e, :], og_t[:, u, e : e + 1], base_t[u][:, e, :], MULT, ADD)
-            nc.sync.dma_start(out=out[256 * u : 256 * (u + 1), :].rearrange("(p e) c -> p e c", e=2), in_=res[:])
+        left0 = minus_one_times("left0", tt0, c0_0[:].rearrange("p a b -> p (a b)"))
+        right0 = minus_one_times("right0", ht0, flat(xs0))
+        xds0 = sb("xds0", [P, 2, 2, P])
+        nc.gpsimd.tensor_tensor(flat(xds0), left0[:], right0[:], MULT)
+        xs1 = turn_forward("xs_prod1", "E", 1, ta1, xs_factors, cos1, sin1, reuse="tt0")
+        woq1 = quantize("wo_1", wo_bf1)
+        c0_1 = product("H", dyq, woq1, FP8X4)
+        angles1 = angles_to_slot_layout(cos1, sin1)
 
-        w1b0 = cast_dealt("w1_0", w1_raw[0])
-        sc0 = gather("sc0", scales_win[0], offs_t, U8)
-        w1q0 = quantize("w1_0", w1b0)
-        wd0 = gather("wd0", words_win[0], offs_t, U16)
-        a0 = first_layer(w1q0, wd0, sc0)
-        c_0 = gather("c_0", cos_win[0], offs2_t, F32)
-        s_0 = gather("s_0", sin_win[0], offs2_t, F32)
-        sc1 = gather("sc1", scales_win[1], offs_t, U8)
-        wd1 = gather("wd1", words_win[1], offs_t, U16)
-        t0 = first_layer(w1q0, wd1, sc1)
-        h0 = forward("fa0", 0, 0, a0, c_0, s_0)
-        w1b1 = cast_dealt("w1_1", w1_raw[1])
-        w1q1 = quantize("w1_1", w1b1)
-        x0 = forward("ft0", 1, 0, t0, c_0, s_0)
-        q0, ht0 = curve(0, h0)
-        a1 = first_layer(w1q1, wd0, sc0)
-        c_1 = gather("c_1", cos_win[1], offs2_t, F32)
-        s_1 = gather("s_1", sin_win[1], offs2_t, F32)
-        t1 = first_layer(w1q1, wd1, sc1)
-        cs0 = turn_angles(c_0, s_0)
-        dyb = cast_plain("dy", dy_raw)
-        wob0 = cast_dealt("wo_0", wo_raw[0])
-        h1 = forward("fa1", 0, 1, a1, c_1, s_1)
-        w20 = m3(0, ht0, x0)
-        dyq = quantize("dy", dyb)
-        woq0 = quantize("wo_0", wob0)
-        c00 = last_layer(dyq, woq0)
-        x1 = forward("ft1", 1, 1, t1, c_1, s_1)
-        q1, ht1 = curve(1, h1)
-        wob1 = cast_dealt("wo_1", wo_raw[1])
-        wa0 = m2(0, q0, c00)
-        xx0 = m4(0, wa0, w20)
-        cs1 = turn_angles(c_1, s_1)
-        woq1 = quantize("wo_1", wob1)
-        c01 = last_layer(dyq, woq1)
-        w21 = m3(1, ht1, x1)
-        wa1 = m2(1, q1, c01)
-        y0 = back(0, xx0, cs0)
-        xx1 = m4(1, wa1, w21)
-        y1 = back(1, xx1, cs1)
-        finish(0, y0)
-        finish(1, y1)
+        t1 = sb("t1", [P, BANK])
+        tt1 = sb("tt1", [P, BANK])
+        ht1 = sb("ht1", [P, BANK])
+        nc.scalar.activation(t1[:], flat(h1), ACT.Tanh)
+        nc.vector.tensor_tensor(ht1[:], flat(h1), t1[:], MULT)
+        nc.scalar.activation(tt1[:], t1[:], ACT.Square)
+        right1 = minus_one_times("right1", ht1, flat(xs1))
+        left1 = minus_one_times("left1", tt1, c0_1[:].rearrange("p a b -> p (a b)"))
+
+        cos_part0 = sb("cos_part0", [P, 2, 2, P])
+        sin_part0 = sb("sin_part0", [P, 2, 2, P])
+        nc.gpsimd.tensor_tensor(cos_part0[:], xds0[:], cos_slot0[:].unsqueeze(2).to_broadcast([P, 2, 2, P]), MULT)
+        nc.gpsimd.tensor_tensor(flat(sin_part0), flat(xds0), flat(sin_slot0), MULT)
+        xda0 = bank("D", [P, 2, J])
+        regions0 = slot_blocks(xda0[:, 0, :]) + slot_blocks(xda0[:, 1, :])
+        transpose_term(regions0, [cos_part0[:, jb, e, :] for e in range(2) for jb in range(2)], opens=True)
+        transpose_term(regions0, [sin_part0[:, jb, 1 - e, :] for e in range(2) for jb in range(2)], closes=True)
+
+        xds1 = sb("xds1", [P, 2, 2, P])
+        nc.vector.tensor_tensor(flat(xds1), left1[:], right1[:], MULT)
+        cos_part1 = sb("cos_part1", [P, 2, 2, P])
+        sin_part1 = [sb("sin_part1_%d" % e, [P, 2, P]) for e in range(2)]
+        nc.vector.tensor_tensor(cos_part1[:], xds1[:], angles1[:, 0, :, :].unsqueeze(2).to_broadcast([P, 2, 2, P]), MULT)
+        nc.vector.tensor_tensor(sin_part1[0][:], xds1[:, :, 1, :], angles1[:, 1, :, :], MULT)
+        nc.vector.scalar_tensor_tensor(sin_part1[1][:], xds1[:, :, 0, :], -1.0, angles1[:, 1, :, :], MULT, MULT)
+        xda1 = [bank(letter, [P, 2, J]) for letter in "AB"]
+        for e in range(2):
+            transpose_term(slot_blocks(xda1[e][:, e, :]), [cos_part1[:, jb, e, :] for jb in range(2)], opens=True)
+            transpose_term(slot_blocks(xda1[e][:, e, :]), [sin_part1[e][:, jb, :] for jb in range(2)], closes=True)
+
+        res0 = sb("res0", [P, 2, J])
+        scaled = sb("scaled", [P, J])
+        nc.scalar.activation(scaled[:], xda0[:, 0, :], ACT.Copy, scale=og_t[:, 0, 0:1])
+        nc.gpsimd.tensor_tensor(res0[:, 0, :], scaled[:], base_t[0][:, 0, :], ADD)
+        add_base(res0, 0, 1, xda0)
+        nc.sync.dma_start(out=half_rows(out, 0), in_=res0[:])
+        res1 = sb("res1", [P, 2, J])
+        for e in range(2):
+            add_base(res1, 1, e, xda1[e])
+            nc.sync.dma_start(out=half_rows(out, 1)[:, e, :], in_=res1[:, e, :])

from contextlib import ExitStack

import concourse.mybir as mybir
from concourse.masks import make_identity

F32 = mybir.dt.float32
BF16 = mybir.dt.bfloat16
I32 = mybir.dt.int32
U32 = mybir.dt.uint32
U16 = mybir.dt.uint16
U8 = mybir.dt.uint8
FP8X4 = mybir.dt.float8_e4m3fn_x4
FP4X4 = mybir.dt.float4_e2m1fn_x4
MULT = mybir.AluOpType.mult
ADD = mybir.AluOpType.add
SUB = mybir.AluOpType.subtract
ACT = mybir.ActivationFunctionType

P = 128
PACK = 4
K, R, T, J, U = 512, 512, 2048, 256, 512
HALF = R // 2
SCALE_ROWS = K // 32
BANK = 512

FLOPS = 3 * 2 * K * R * J


def tile_attend_hvturned_kernel(
    tc, tab_words, tab_scales, w1, cosn, sinn, gain, wo, dy, dtab_words, dtab_scales, og, base, offs, offs2, out
):
    nc = tc.nc
    with ExitStack() as ctx:
        keep = ctx.enter_context(tc.tile_pool(name="keep", bufs=1))
        psum = ctx.enter_context(tc.psum_pool(name="psum", bufs=1))

        def sb(name, shape, dtype=F32, reuse=None):
            return keep.tile(shape, dtype, name=name, tag=reuse or name, align_bytes=64)

        def bank(letter, shape):
            return psum.tile(shape, F32, name="bank" + letter, tag="bank" + letter)

        def flat(tile):
            return tile[:].rearrange("p a b c -> p (a b c)")

        def half_rows(src, u):
            return src[HALF * u : HALF * (u + 1), :].rearrange("(p e) c -> p e c", e=2)

        offs_t = keep.tile([P, J // 16], U16, name="offs_t")
        offs2_t = keep.tile([P, J // 16], U16, name="offs2_t")
        words_win = [sb("words_win%d" % i, [P, T], U16) for i in range(2)]
        scales_win = [sb("scales_win%d" % i, [P, T], U8) for i in range(2)]
        cos_win = [sb("cos_win%d" % u, [P, U]) for u in range(2)]
        sin_win = [sb("sin_win%d" % u, [P, U]) for u in range(2)]
        w1_raw = [sb("w1_raw%d" % u, [P, PACK, HALF]) for u in range(2)]
        wo_raw = [sb("wo_raw%d" % u, [P, PACK, HALF]) for u in range(2)]
        dy_raw = sb("dy_raw", [P, PACK, J])
        base_t = [sb("base%d" % u, [P, 2, J]) for u in range(2)]
        gain_t = sb("gain_t", [P, 2, 2])
        og_t = sb("og_t", [P, 2, 2])
        ident = sb("ident", [P, P])

        nc.gpsimd.memset(scales_win[0][:].bitcast(I32), 0)
        nc.vector.memset(scales_win[1][:].bitcast(I32), 0)

        def load_words(i, src):
            nc.sync.dma_start(out=words_win[i][:].bitcast(I32), in_=src[0].bitcast(I32))

        def load_scales(i, src):
            for r in range(4):
                nc.sync.dma_start(out=scales_win[i][r:P:32, :].bitcast(I32), in_=src[0, r:SCALE_ROWS:4, :].bitcast(I32))

        def load_operand(dst, src):
            nc.sync.dma_start(out=dst[:], in_=src.rearrange("(p j) c -> p j c", j=PACK))

        def load_weights(dst, src, u):
            load_operand(dst[u], src[:, HALF * u : HALF * (u + 1)])

        def load_angles(dst, src, u):
            nc.sync.dma_start(out=dst[u][:], in_=half_rows(src, u)[:, 0, :])

        def load_per_feature(dst, src):
            nc.sync.dma_start(out=dst[:], in_=src.rearrange("(u p e) o -> p u (e o)", u=2, e=2))

        nc.sync.dma_start(offs_t[:], offs)
        nc.sync.dma_start(offs2_t[:], offs2)
        load_scales(0, tab_scales)
        make_identity(nc, ident[:])
        load_weights(w1_raw, w1, 0)
        load_words(0, tab_words)
        load_scales(1, dtab_scales)
        load_per_feature(gain_t, gain)
        load_words(1, dtab_words)
        load_angles(cos_win, cosn, 0)
        load_angles(sin_win, sinn, 0)
        load_weights(w1_raw, w1, 1)
        load_operand(dy_raw, dy)
        load_weights(wo_raw, wo, 0)
        load_angles(cos_win, cosn, 1)
        load_angles(sin_win, sinn, 1)
        load_weights(wo_raw, wo, 1)
        load_per_feature(og_t, og)
        for u in range(2):
            nc.sync.dma_start(out=base_t[u][:], in_=half_rows(base, u))

        def gain_factors():
            lin, neg_lin, sq, neg_sq = [sb(name, [P, 2, 2]) for name in ("lin", "neg_lin", "sq", "neg_sq")]
            nc.scalar.activation(lin[:], gain_t[:], ACT.Copy, scale=0.5)
            nc.scalar.activation(neg_lin[:], gain_t[:], ACT.Copy, scale=-0.5)
            nc.scalar.activation(sq[:], gain_t[:], ACT.Square, scale=0.5**0.5)
            nc.scalar.activation(neg_sq[:], sq[:], ACT.Copy, scale=-1.0)
            return (lin, neg_lin), (sq, neg_sq)

        def cast_weights(name, raw):
            grouped = sb(name + "_bf", [P, PACK * HALF], BF16)
            nc.scalar.copy(
                grouped[:].rearrange("p (e m i j) -> p m j i e", e=2, i=2, j=PACK),
                raw[:].rearrange("p j (m i e) -> p m j i e", i=2, e=2),
            )
            return grouped

        def cast_dy():
            grouped = sb("dy_bf", [P, PACK * J], BF16)
            nc.scalar.copy(
                grouped[:].rearrange("p (c i j) -> p c j i", i=4, j=PACK),
                dy_raw[:].rearrange("p j (c i) -> p c j i", i=4),
            )
            return grouped

        def quantize(name, grouped, reuse=None):
            width = grouped.shape[1] // PACK
            codes = sb(name + "_codes", [P, width], U32, reuse)
            scales = sb(name + "_scales", [P, width], U8)
            nc.vector.quantize_mx(out=codes[:].bitcast(FP8X4), scales=scales[:], in_=grouped[:])
            return codes, scales

        def gather(name, window, offsets, dtype):
            got = sb(name, [P, J], dtype)
            nc.vector.tensor_copy(got[:], window[:].indirect(offsets[:]))
            return got

        def product(letter, stationary, moving, moving_dtype):
            acc = bank(letter, [P, 2, BANK // 2])
            for b in range(2):
                cols = slice(P * b, P * (b + 1))
                nc.tensor.matmul_mx(
                    out=acc[:, b, :],
                    lhsT=stationary[0][:, cols].bitcast(FP8X4),
                    lhsT_scale=stationary[1][:, cols],
                    rhs=moving[0][:].bitcast(moving_dtype),
                    rhs_scale=moving[1][:],
                    start=True,
                    stop=True,
                )
            return acc

        def transpose_term(dsts, srcs, opens=False, closes=False):
            last = len(dsts) - 1
            for n, (dst, src) in enumerate(zip(dsts, srcs)):
                nc.tensor.matmul(
                    dst, lhsT=src, rhs=ident[:], is_transpose=True, start=opens and n == 0, stop=closes and n == last
                )

        def slot_blocks(ap):
            return [ap[:, P * jb : P * (jb + 1)] for jb in range(2)]

        def turn_forward(name, letter, u, acc, factors, cos, sin, reuse=None):
            plus, minus = factors
            dst = bank(letter, [P, 2, 2, P])
            prod = sb(name, [P, 2, 2, J], reuse=reuse)
            regions = [[dst[:, jb, e, :] for jb in range(2)] for e in range(2)]
            for e in range(2):
                nc.vector.scalar_tensor_tensor(prod[:, e, 0, :], acc[:, e, :], plus[:, u, e : e + 1], cos[:], MULT, MULT)
                transpose_term(regions[e], slot_blocks(prod[:, e, 0, :]), opens=e == 0)
            for e, sin_factor in enumerate((minus, plus)):
                nc.vector.scalar_tensor_tensor(
                    prod[:, e, 1, :], acc[:, 1 - e, :], sin_factor[:, u, e : e + 1], sin[:], MULT, MULT
                )
                transpose_term(regions[e], slot_blocks(prod[:, e, 1, :]), closes=e == 1)
            return dst

        def angles_to_slot_layout(cos, sin):
            dst = bank("G", [P, 2, 2, P])
            for k, src in enumerate((cos, sin)):
                for jb, block in enumerate(slot_blocks(src)):
                    nc.tensor.transpose(dst[:, k, jb, :], block, ident[:])
            return dst

        def minus_one_times(name, tile, acc):
            dst = sb(name, [P, BANK])
            nc.vector.scalar_tensor_tensor(dst[:], tile[:], 1.0, acc, SUB, MULT)
            return dst

        def add_base(res, u, e, xda):
            nc.vector.scalar_tensor_tensor(res[:, e, :], xda[:, e, :], og_t[:, u, e : e + 1], base_t[u][:, e, :], MULT, ADD)

        tab_sc = gather("tab_sc", scales_win[0], offs_t, U8)
        w1_bf0 = cast_weights("w1_0", w1_raw[0])
        h_factors, xs_factors = gain_factors()
        tab = (gather("tab_wd", words_win[0], offs_t, U16), tab_sc)
        w1q0 = quantize("w1_0", w1_bf0)
        a0 = product("A", w1q0, tab, FP4X4)
        dtab_sc = gather("dtab_sc", scales_win[1], offs_t, U8)
        dtab = (gather("dtab_wd", words_win[1], offs_t, U16), dtab_sc)
        ta0 = product("B", w1q0, dtab, FP4X4)
        cos0 = gather("cos0", cos_win[0], offs2_t, F32)
        sin0 = gather("sin0", sin_win[0], offs2_t, F32)
        h0 = turn_forward("h_prod0", "C", 0, a0, h_factors, cos0, sin0)
        w1_bf1 = cast_weights("w1_1", w1_raw[1])
        xs0 = turn_forward("xs_prod0", "D", 0, ta0, xs_factors, cos0, sin0)

        w1q1 = quantize("w1_1", w1_bf1)
        a1 = product("A", w1q1, tab, FP4X4)
        ta1 = product("B", w1q1, dtab, FP4X4)
        angles0 = angles_to_slot_layout(cos0, sin0)
        dy_bf = cast_dy()
        wo_bf0 = cast_weights("wo_0", wo_raw[0])

        t_and_h0 = sb("t_and_h0", [P, 2, BANK], reuse="wo_raw0")
        tt0 = sb("tt0", [P, BANK])
        ht0 = sb("ht0", [P, BANK])
        nc.scalar.activation(t_and_h0[:, 0, :], flat(h0), ACT.Tanh)
        nc.scalar.copy(t_and_h0[:, 1, :], flat(h0))
        nc.gpsimd.tensor_tensor(ht0[:], t_and_h0[:, 1, :], t_and_h0[:, 0, :], MULT)
        nc.scalar.activation(tt0[:], t_and_h0[:, 0, :], ACT.Square)

        dyq = quantize("dy", dy_bf)
        cos1 = gather("cos1", cos_win[1], offs2_t, F32)
        woq0 = quantize("wo_0", wo_bf0, reuse="cos_win1")
        c0_0 = product("F", dyq, woq0, FP8X4)
        sin1 = gather("sin1", sin_win[1], offs2_t, F32)
        h1 = turn_forward("h_prod1", "C", 1, a1, h_factors, cos1, sin1, reuse="wo_0_bf")
        wo_bf1 = cast_weights("wo_1", wo_raw[1])

        cos_slot0 = sb("cos_slot0", [P, 2, P], reuse="wo_raw0")
        sin_slot0 = sb("sin_slot0", [P, 2, 2, P], reuse="wo_raw1")
        nc.scalar.copy(cos_slot0[:], angles0[:, 0, :, :])
        nc.scalar.activation(sin_slot0[:, :, 0, :], angles0[:, 1, :, :], ACT.Copy, scale=-1.0)
        nc.scalar.copy(sin_slot0[:, :, 1, :], angles0[:, 1, :, :])

        left0 = minus_one_times("left0", tt0, c0_0[:].rearrange("p a b -> p (a b)"))
        right0 = minus_one_times("right0", ht0, flat(xs0))
        xds0 = sb("xds0", [P, 2, 2, P])
        nc.gpsimd.tensor_tensor(flat(xds0), left0[:], right0[:], MULT)
        xs1 = turn_forward("xs_prod1", "E", 1, ta1, xs_factors, cos1, sin1, reuse="tt0")
        woq1 = quantize("wo_1", wo_bf1)
        c0_1 = product("H", dyq, woq1, FP8X4)
        angles1 = angles_to_slot_layout(cos1, sin1)

        t1 = sb("t1", [P, BANK])
        tt1 = sb("tt1", [P, BANK])
        ht1 = sb("ht1", [P, BANK])
        nc.scalar.activation(t1[:], flat(h1), ACT.Tanh)
        nc.vector.tensor_tensor(ht1[:], flat(h1), t1[:], MULT)
        nc.scalar.activation(tt1[:], t1[:], ACT.Square)
        right1 = minus_one_times("right1", ht1, flat(xs1))
        left1 = minus_one_times("left1", tt1, c0_1[:].rearrange("p a b -> p (a b)"))

        cos_part0 = sb("cos_part0", [P, 2, 2, P])
        sin_part0 = sb("sin_part0", [P, 2, 2, P])
        nc.gpsimd.tensor_tensor(cos_part0[:], xds0[:], cos_slot0[:].unsqueeze(2).to_broadcast([P, 2, 2, P]), MULT)
        nc.gpsimd.tensor_tensor(flat(sin_part0), flat(xds0), flat(sin_slot0), MULT)
        xda0 = bank("D", [P, 2, J])
        regions0 = slot_blocks(xda0[:, 0, :]) + slot_blocks(xda0[:, 1, :])
        transpose_term(regions0, [cos_part0[:, jb, e, :] for e in range(2) for jb in range(2)], opens=True)
        transpose_term(regions0, [sin_part0[:, jb, 1 - e, :] for e in range(2) for jb in range(2)], closes=True)

        xds1 = sb("xds1", [P, 2, 2, P])
        nc.vector.tensor_tensor(flat(xds1), left1[:], right1[:], MULT)
        cos_part1 = sb("cos_part1", [P, 2, 2, P])
        sin_part1 = [sb("sin_part1_%d" % e, [P, 2, P]) for e in range(2)]
        nc.vector.tensor_tensor(cos_part1[:], xds1[:], angles1[:, 0, :, :].unsqueeze(2).to_broadcast([P, 2, 2, P]), MULT)
        nc.vector.tensor_tensor(sin_part1[0][:], xds1[:, :, 1, :], angles1[:, 1, :, :], MULT)
        nc.vector.scalar_tensor_tensor(sin_part1[1][:], xds1[:, :, 0, :], -1.0, angles1[:, 1, :, :], MULT, MULT)
        xda1 = [bank(letter, [P, 2, J]) for letter in "AB"]
        for e in range(2):
            transpose_term(slot_blocks(xda1[e][:, e, :]), [cos_part1[:, jb, e, :] for jb in range(2)], opens=True)
            transpose_term(slot_blocks(xda1[e][:, e, :]), [sin_part1[e][:, jb, :] for jb in range(2)], closes=True)

        res0 = sb("res0", [P, 2, J])
        scaled = sb("scaled", [P, J])
        nc.scalar.activation(scaled[:], xda0[:, 0, :], ACT.Copy, scale=og_t[:, 0, 0:1])
        nc.gpsimd.tensor_tensor(res0[:, 0, :], scaled[:], base_t[0][:, 0, :], ADD)
        add_base(res0, 0, 1, xda0)
        nc.sync.dma_start(out=half_rows(out, 0), in_=res0[:])
        res1 = sb("res1", [P, 2, J])
        for e in range(2):
            add_base(res1, 1, e, xda1[e])
            nc.sync.dma_start(out=half_rows(out, 1)[:, e, :], in_=res1[:, e, :])
